import numpy as np
import ml_dtypes


def mxq(x, axis, fmt="e4m3"):
    dtype, down = {"e4m3": (ml_dtypes.float8_e4m3fn, 7), "e5m2": (ml_dtypes.float8_e5m2, 14)}[fmt]
    v = np.moveaxis(np.asarray(x, np.float32).astype(ml_dtypes.bfloat16).astype(np.float64), axis, -1)
    blocks = v.reshape(v.shape[:-1] + (-1, 32))
    amax = np.abs(blocks).max(-1, keepdims=True)
    byte = np.maximum(np.where(amax > 0, np.frexp(amax)[1] - 1 + 127, 0) - down, 1)
    scale = np.exp2(byte - 127.0)
    codes = (blocks / scale).astype(np.float32).astype(dtype).astype(np.float64)
    return np.moveaxis((codes * scale).reshape(v.shape), -1, axis)


WIDE = False


def mx_kscale(k):
    if not WIDE:
        return np.ones(k)
    levels = np.array([30, -30])
    if k % 512:
        return np.exp2(np.random.permutation(np.resize(levels, k // 32))).repeat(32)
    a = np.empty((k // 512, 16))
    for p in range(k // 512):
        a[p, :8] = np.random.permutation(np.resize(levels, 8))
        for g in range(8):
            far = levels[np.abs(levels - a[p, g]) >= 10]
            a[p, g + 8] = far[np.random.randint(len(far))]
    return np.exp2(a.ravel()).repeat(32)


def f64(x):
    return np.asarray(x).astype(np.float64)


def striped(idx):
    return np.tile(np.asarray(idx).reshape(-1, 16).T, (8, 1)).astype(np.uint16)


def unstriped(offs):
    return offs[:16].T.reshape(-1).astype(np.int64)


E2M1 = np.array([0.0, 0.5, 1.0, 1.5, 2.0, 3.0, 4.0, 6.0, -0.0, -0.5, -1.0, -1.5, -2.0, -3.0, -4.0, -6.0])


def pack_weight(w, fmt):
    k, n = w.shape
    w = f64(np.asarray(w, np.float32).astype(ml_dtypes.bfloat16)).reshape(k // 32, 32, n)
    amax = np.abs(w).max(1)
    if fmt in ("e4m3", "e5m2"):
        byte = np.frexp(amax)[1] - 1 + 127 - (7 if fmt == "e4m3" else 14)
    else:
        mant, ex = np.frexp(amax / 6.0)
        byte = np.where(mant > 0.5, ex, ex - 1) + 127
    byte = np.clip(np.where(amax > 0, byte, 1), 1, 254)
    scaled = (w * np.exp2(127.0 - byte)[:, None, :]).reshape(k, n).astype(np.float32)
    by_word = np.ascontiguousarray(scaled.reshape(k // 512, 128, 4, n).transpose(0, 1, 3, 2))
    if fmt in ("e4m3", "e5m2"):
        words = by_word.astype(ml_dtypes.float8_e4m3fn if fmt == "e4m3" else ml_dtypes.float8_e5m2).view(np.uint8)
    else:
        c = by_word.astype(ml_dtypes.float4_e2m1fn).view(np.uint8) & 0xF
        words = (c[..., 0::2] | (c[..., 1::2] << 4)).reshape(k // 512, 128, 2 * n)
    return np.ascontiguousarray(words), np.ascontiguousarray(byte.astype(np.uint8).reshape(k // 512, 16, n))


def unpack_weight(words, scales, fmt):
    g, _, n = scales.shape
    words = np.ascontiguousarray(words).reshape(g, 128, n, -1)
    if fmt in ("e4m3", "e5m2"):
        vals = words.view(ml_dtypes.float8_e4m3fn if fmt == "e4m3" else ml_dtypes.float8_e5m2).astype(np.float64)
    else:
        nib = np.empty((g, 128, n, 4), np.uint8)
        nib[..., 0::2] = words & 0xF
        nib[..., 1::2] = words >> 4
        vals = E2M1[nib]
    vals = vals * np.repeat(np.exp2(scales.astype(np.float64) - 127.0), 8, axis=1)[..., None]
    return vals.transpose(0, 1, 3, 2).reshape(g * 512, n)


K, T, J, I, R, C, S = 512, 512, 256, 256, 512, 512, 64


def setup_inputs():
    n = np.random.standard_normal
    idx = np.random.permutation(T)[:J]
    idx2 = np.random.permutation(C)[:J]
    idx3 = np.random.permutation(T)[:I]
    fk = mx_kscale(K)
    fr = mx_kscale(R)
    xtp = pack_weight(n((K, T)) / fk[:, None], "e5m2")
    wap = pack_weight(n((K, R)) * 0.5 / np.sqrt(K) * fk[:, None] * fr, "e4m3")
    wbp = pack_weight(n((K, R)) * 1 / np.sqrt(K) * fk[:, None] / fr, "e2m1")
    return {
        "xt_words": xtp[0],
        "xt_scales": xtp[1],
        "wa_words": wap[0],
        "wa_scales": wap[1],
        "tf": (n((R, C))).astype(np.float32),
        "wb_words": wbp[0],
        "wb_scales": wbp[1],
        "cw1": (np.random.uniform(-1.0, 1.0, (1, I))).astype(np.float32),
        "offs": striped(idx),
        "offs2": striped(idx2),
        "offs3": striped(idx3),
    }


def reference(xt_words, xt_scales, wa_words, wa_scales, tf, wb_words, wb_scales, cw1, offs, offs2, offs3):
    idx = unstriped(offs)
    idx2 = unstriped(offs2)
    idx3 = unstriped(offs3)
    xtu = unpack_weight(xt_words, xt_scales, "e5m2")
    wau = unpack_weight(wa_words, wa_scales, "e4m3")
    wbu = unpack_weight(wb_words, wb_scales, "e2m1")
    xtidxg = xtu[:, idx]
    za = wau.T @ xtidxg
    ha = za * f64(tf)[:, idx2]
    xtidx3g = xtu[:, idx3]
    zb = wbu.T @ xtidx3g
    kb1 = np.max(zb, axis=1, keepdims=True)
    hb = np.maximum(zb - 0.4 * kb1, 0.0)
    haq = mxq(ha, 0, "e5m2")
    hbq = mxq(hb, 0, "e4m3")
    a0 = haq.T @ hbq
    y = 0.04 * (a0 * f64(cw1)).reshape(J, S, I // S).sum(axis=2)
    return y

@@ -1,0 +1,183 @@
+from contextlib import ExitStack
+
+import concourse.mybir as mybir
+
+K, T, J, I, R, C, S = 512, 512, 256, 256, 512, 512, 64
+FLOPS = 2 * K * R * J + 2 * K * R * I + 2 * R * J * I
+
+F32 = mybir.dt.float32
+BF16 = mybir.dt.bfloat16
+I32 = mybir.dt.int32
+U32 = mybir.dt.uint32
+U16 = mybir.dt.uint16
+U8 = mybir.dt.uint8
+E4M3 = mybir.dt.float8_e4m3fn_x4
+E5M2 = mybir.dt.float8_e5m2_x4
+E2M1 = mybir.dt.float4_e2m1fn_x4
+ALU = mybir.AluOpType
+ACT = mybir.ActivationFunctionType
+
+P = 128
+PACK = 4
+RUN = 8
+HALF = 128
+
+
+def tile_list_meet_timestable_peakgated_summed_kernel(
+    tc, xt_words, xt_scales, wa_words, wa_scales, tf, wb_words, wb_scales, cw1, offs, offs2, offs3, out
+):
+    nc = tc.nc
+    with ExitStack() as ctx:
+        lists = ctx.enter_context(tc.tile_pool(name="lists", bufs=1))
+        sb = ctx.enter_context(tc.tile_pool(name="sb", bufs=1))
+        ps = ctx.enter_context(tc.psum_pool(name="ps", bufs=1))
+
+        def load_scale_rows(queue, plane, scales):
+            rows = scales[0].bitcast(I32)
+            for q in range(4):
+                queue.dma_start(
+                    out=plane[32 * q : 32 * (q + 1), :].bitcast(I32),
+                    in_=rows[4 * q : 4 * q + 4, :].partition_broadcast(8),
+                )
+
+        def deal(dst, src, run):
+            nc.vector.tensor_copy(
+                out=dst[:].bitcast(I32).rearrange("p (t q s) -> p t q s", t=PACK, s=run),
+                in_=src[:].bitcast(I32).rearrange("p (q t s) -> p t q s", t=PACK, s=run),
+            )
+
+        list_a = lists.tile([P, J // 16], U16, name="list_a")
+        list_f = lists.tile([P, J // 16], U16, name="list_f")
+        list_b = lists.tile([P, I // 16], U16, name="list_b")
+
+        xs = sb.tile([P, T], U8, name="xs", align_bytes=64)
+        wbs_raw = sb.tile([P, R], U8, name="wbs_raw", align_bytes=64)
+        was_raw = sb.tile([P, R], U8, name="was_raw", align_bytes=64)
+
+        xw = sb.tile([P, T], U32, name="xw", align_bytes=64)
+        wbw_raw = sb.tile([P, 2 * R], U8, name="wbw_raw", align_bytes=64)
+        waw_raw = sb.tile([P, R], U32, name="waw_raw", align_bytes=64)
+        tf_rows = [sb.tile([P, C], F32, name="tf_rows%d" % t, align_bytes=64) for t in range(PACK)]
+        cw = sb.tile([P, I], F32, name="cw", align_bytes=64)
+
+        nc.sync.dma_start(list_b[:], offs3)
+        tf_by_slot = tf.rearrange("(q t s) c -> t q s c", t=PACK, s=RUN)
+        for t in range(2):
+            nc.gpsimd.dma_start(out=tf_rows[t][:], in_=tf_by_slot[t])
+        nc.sync.dma_start(out=xw[:].bitcast(I32), in_=xt_words[0].rearrange("p n t -> p (n t)").bitcast(I32))
+        load_scale_rows(nc.scalar, xs, xt_scales)
+        nc.sync.dma_start(list_a[:], offs)
+        nc.sync.dma_start(list_f[:], offs2)
+        load_scale_rows(nc.sync, wbs_raw, wb_scales)
+        nc.sync.dma_start(out=wbw_raw[:].bitcast(I32), in_=wb_words[0].bitcast(I32))
+        nc.sync.dma_start(out=waw_raw[:].bitcast(I32), in_=wa_words[0].rearrange("p n t -> p (n t)").bitcast(I32))
+        for t in range(2, PACK):
+            nc.sync.dma_start(out=tf_rows[t][:], in_=tf_by_slot[t])
+        load_scale_rows(nc.sync, was_raw, wa_scales)
+        nc.sync.dma_start(out=cw[:], in_=cw1[0].partition_broadcast(P))
+
+        xw_b = sb.tile([P, I], U32, name="xw_b", align_bytes=64)
+        xs_b = sb.tile([P, I], U8, name="xs_b", align_bytes=64)
+        nc.vector.tensor_copy(xw_b[:], xw[:].indirect(list_b[:]))
+        nc.vector.tensor_copy(xs_b[:], xs[:].indirect(list_b[:]))
+        wbw = sb.tile([P, 2 * R], U8, name="wbw", align_bytes=64)
+        wbs = sb.tile([P, R], U8, name="wbs", align_bytes=64)
+        deal(wbw, wbw_raw, RUN // 2)
+        deal(wbs, wbs_raw, RUN // 4)
+        zb = [ps.tile([P, 2, I], F32, name="zb%d" % b) for b in range(2)]
+        for t in range(PACK):
+            nc.tensor.matmul_mx(
+                out=zb[t // 2][:, t % 2, :],
+                lhsT=wbw[:, 2 * P * t : 2 * P * (t + 1)].bitcast(E2M1),
+                lhsT_scale=wbs[:, P * t : P * (t + 1)],
+                rhs=xw_b[:].bitcast(E5M2),
+                rhs_scale=xs_b[:],
+                start=True,
+                stop=True,
+            )
+
+        xw_a = sb.tile([P, J], U32, name="xw_a", align_bytes=64)
+        xs_a = sb.tile([P, J], U8, name="xs_a", align_bytes=64)
+        nc.vector.tensor_copy(xw_a[:], xw[:].indirect(list_a[:]))
+        nc.vector.tensor_copy(xs_a[:], xs[:].indirect(list_a[:]))
+        waw = sb.tile([P, R], U32, name="waw", align_bytes=64)
+        was = sb.tile([P, R], U8, name="was", align_bytes=64)
+        deal(waw, waw_raw, RUN)
+        deal(was, was_raw, RUN // 4)
+        za = [ps.tile([P, PACK, HALF], F32, name="za%d" % h) for h in range(2)]
+        for h in range(2):
+            cols = slice(HALF * h, HALF * (h + 1))
+            for t in range(PACK):
+                nc.tensor.matmul_mx(
+                    out=za[h][:, t, :],
+                    lhsT=waw[:, P * t : P * (t + 1)].bitcast(E4M3),
+                    lhsT_scale=was[:, P * t : P * (t + 1)],
+                    rhs=xw_a[:, cols].bitcast(E5M2),
+                    rhs_scale=xs_a[:, cols],
+                    start=True,
+                    stop=True,
+                )
+
+        tf_picked = sb.tile([P, PACK, J], F32, name="tf_picked", align_bytes=64)
+        for t in range(PACK):
+            nc.scalar.activation(tf_picked[:, t, :], tf_rows[t][:].indirect(list_f[:]), ACT.Copy)
+
+        peak = [sb.tile([P, 2], F32, name="peak%d" % b) for b in range(2)]
+        bias = [sb.tile([P, 2], F32, name="bias%d" % b) for b in range(2)]
+        hb_slots = sb.tile([P, PACK, I], BF16, name="hb_slots", align_bytes=64)
+        for b in range(2):
+            nc.vector.tensor_reduce(out=peak[b][:], in_=zb[b][:], axis=mybir.AxisListType.X, op=ALU.max)
+        for b in range(2):
+            nc.scalar.activation(bias[b][:], peak[b][:], ACT.Copy, scale=-0.4)
+            for u in range(2):
+                nc.scalar.activation(
+                    hb_slots[:, 2 * b + u, :], zb[b][:, u, :], ACT.Relu, bias=bias[b][:, u : u + 1], scale=1.0
+                )
+
+        ha = [sb.tile([P, HALF, PACK], BF16, name="ha%d" % h, align_bytes=64) for h in range(2)]
+        ha_codes = [sb.tile([P, HALF], U32, name="ha_codes%d" % h, align_bytes=64) for h in range(2)]
+        ha_scales = [sb.tile([P, HALF], U8, name="ha_scales%d" % h, align_bytes=64) for h in range(2)]
+        for h in range(2):
+            nc.vector.tensor_tensor(
+                out=ha[h][:],
+                in0=za[h][:].rearrange("p t j -> p j t"),
+                in1=tf_picked[:, :, HALF * h : HALF * (h + 1)].rearrange("p t j -> p j t"),
+                op=ALU.mult,
+            )
+        hb = sb.tile([P, I, PACK], BF16, name="hb", align_bytes=64)
+        hb_codes = sb.tile([P, I], U32, name="hb_codes", align_bytes=64)
+        hb_scales = sb.tile([P, I], U8, name="hb_scales", align_bytes=64)
+        nc.vector.tensor_copy(out=hb[:], in_=hb_slots[:].rearrange("p t i -> p i t"))
+        for h in range(2):
+            nc.vector.quantize_mx(
+                out=ha_codes[h][:].bitcast(E5M2), scales=ha_scales[h][:], in_=ha[h][:].rearrange("p j t -> p (j t)")
+            )
+        nc.vector.quantize_mx(
+            out=hb_codes[:].bitcast(E4M3), scales=hb_scales[:], in_=hb[:].rearrange("p i t -> p (i t)")
+        )
+
+        a0 = [ps.tile([P, I], F32, name="a0_%d" % h) for h in range(2)]
+        weighted = [sb.tile([P, S, I // S], F32, name="weighted%d" % h) for h in range(2)]
+        res = [sb.tile([P, S], F32, name="res%d" % h) for h in range(2)]
+        for h in range(2):
+            nc.tensor.matmul_mx(
+                out=a0[h][:],
+                lhsT=ha_codes[h][:].bitcast(E5M2),
+                lhsT_scale=ha_scales[h][:],
+                rhs=hb_codes[:].bitcast(E4M3),
+                rhs_scale=hb_scales[:],
+                start=True,
+                stop=True,
+            )
+        for h in range(2):
+            nc.vector.scalar_tensor_tensor(
+                out=weighted[h][:].rearrange("p s u -> p (s u)"),
+                in0=a0[h][:],
+                scalar=0.04,
+                in1=cw[:],
+                op0=ALU.mult,
+                op1=ALU.mult,
+            )
+        for h in range(2):
+            nc.vector.tensor_reduce(out=res[h][:], in_=weighted[h][:], axis=mybir.AxisListType.X, op=ALU.add)
+            nc.sync.dma_start(out=out[HALF * h : HALF * (h + 1), :], in_=res[h][:])

@@ -35,10 +35,7 @@ def tile_list_meet_timestable_peakgated_summed_kernel(
         def load_scale_rows(queue, plane, scales):
             rows = scales[0].bitcast(I32)
             for q in range(4):
-                queue.dma_start(
-                    out=plane[32 * q : 32 * (q + 1), :].bitcast(I32),
-                    in_=rows[4 * q : 4 * q + 4, :].partition_broadcast(8),
-                )
+                queue.dma_start(out=plane[32 * q : 32 * q + 4, :].bitcast(I32), in_=rows[4 * q : 4 * q + 4, :])
 
         def deal(dst, src, run):
             nc.vector.tensor_copy(
@@ -52,7 +49,11 @@ def tile_list_meet_timestable_peakgated_summed_kernel(
 
         xs = sb.tile([P, T], U8, name="xs", align_bytes=64)
         wbs_raw = sb.tile([P, R], U8, name="wbs_raw", align_bytes=64)
-        was_raw = sb.tile([P, R], U8, name="was_raw", align_bytes=64)
+        was_raw = sb.tile([P, R], U8, name="was_raw", tag="reused", align_bytes=64)
+
+        nc.gpsimd.memset(xs[:].bitcast(I32), 0)
+        nc.vector.memset(wbs_raw[:].bitcast(I32), 0)
+        nc.vector.memset(was_raw[:].bitcast(I32), 0)
 
         xw = sb.tile([P, T], U32, name="xw", align_bytes=64)
         wbw_raw = sb.tile([P, 2 * R], U8, name="wbw_raw", align_bytes=64)
@@ -70,9 +71,9 @@ def tile_list_meet_timestable_peakgated_summed_kernel(
         nc.sync.dma_start(list_f[:], offs2)
         load_scale_rows(nc.sync, wbs_raw, wb_scales)
         nc.sync.dma_start(out=wbw_raw[:].bitcast(I32), in_=wb_words[0].bitcast(I32))
+        nc.sync.dma_start(out=tf_rows[2][:], in_=tf_by_slot[2])
         nc.sync.dma_start(out=waw_raw[:].bitcast(I32), in_=wa_words[0].rearrange("p n t -> p (n t)").bitcast(I32))
-        for t in range(2, PACK):
-            nc.sync.dma_start(out=tf_rows[t][:], in_=tf_by_slot[t])
+        nc.sync.dma_start(out=tf_rows[3][:], in_=tf_by_slot[3])
         load_scale_rows(nc.sync, was_raw, wa_scales)
         nc.sync.dma_start(out=cw[:], in_=cw1[0].partition_broadcast(P))
 
@@ -81,13 +82,13 @@ def tile_list_meet_timestable_peakgated_summed_kernel(
         nc.vector.tensor_copy(xw_b[:], xw[:].indirect(list_b[:]))
         nc.vector.tensor_copy(xs_b[:], xs[:].indirect(list_b[:]))
         wbw = sb.tile([P, 2 * R], U8, name="wbw", align_bytes=64)
-        wbs = sb.tile([P, R], U8, name="wbs", align_bytes=64)
+        wbs = sb.tile([P, R], U8, name="wbs", tag="reused2", align_bytes=64)
         deal(wbw, wbw_raw, RUN // 2)
         deal(wbs, wbs_raw, RUN // 4)
-        zb = [ps.tile([P, 2, I], F32, name="zb%d" % b) for b in range(2)]
+        zb = [ps.tile([P, I], F32, name="zb%d" % t) for t in range(PACK)]
         for t in range(PACK):
             nc.tensor.matmul_mx(
-                out=zb[t // 2][:, t % 2, :],
+                out=zb[t][:],
                 lhsT=wbw[:, 2 * P * t : 2 * P * (t + 1)].bitcast(E2M1),
                 lhsT_scale=wbs[:, P * t : P * (t + 1)],
                 rhs=xw_b[:].bitcast(E5M2),
@@ -101,8 +102,27 @@ def tile_list_meet_timestable_peakgated_summed_kernel(
         nc.vector.tensor_copy(xw_a[:], xw[:].indirect(list_a[:]))
         nc.vector.tensor_copy(xs_a[:], xs[:].indirect(list_a[:]))
         waw = sb.tile([P, R], U32, name="waw", align_bytes=64)
-        was = sb.tile([P, R], U8, name="was", align_bytes=64)
         deal(waw, waw_raw, RUN)
+        tf_picked = sb.tile([P, PACK, J], F32, name="tf_picked", align_bytes=64)
+        for t in range(2):
+            nc.scalar.activation(tf_picked[:, t, :], tf_rows[t][:].indirect(list_f[:]), ACT.Copy)
+
+        neg_peak = [tf_picked[:, 2, 0:1], tf_picked[:, 3, 0:1], tf_picked[:, 2, 128:129], tf_picked[:, 3, 128:129]]
+        hb_slots = sb.tile([P, PACK, I], F32, name="hb_slots", align_bytes=64)
+        for t in range(PACK):
+            nc.vector.tensor_reduce(
+                out=neg_peak[t], in_=zb[t][:], axis=mybir.AxisListType.X, op=ALU.max, negate=True
+            )
+            nc.scalar.activation(hb_slots[:, t, :], zb[t][:], ACT.Relu, bias=neg_peak[t], scale=2.5)
+        for h in range(2):
+            for t in range(2, PACK):
+                nc.scalar.activation(
+                    tf_picked[:, t, HALF * h : HALF * (h + 1)],
+                    tf_rows[t][:].indirect(list_f[:, 8 * h : 8 * (h + 1)]),
+                    ACT.Copy,
+                )
+
+        was = sb.tile([P, R], U8, name="was", tag="reused2", align_bytes=64)
         deal(was, was_raw, RUN // 4)
         za = [ps.tile([P, PACK, HALF], F32, name="za%d" % h) for h in range(2)]
         for h in range(2):
@@ -118,43 +138,40 @@ def tile_list_meet_timestable_peakgated_summed_kernel(
                     stop=True,
                 )
 
-        tf_picked = sb.tile([P, PACK, J], F32, name="tf_picked", align_bytes=64)
-        for t in range(PACK):
-            nc.scalar.activation(tf_picked[:, t, :], tf_rows[t][:].indirect(list_f[:]), ACT.Copy)
-
-        peak = [sb.tile([P, 2], F32, name="peak%d" % b) for b in range(2)]
-        bias = [sb.tile([P, 2], F32, name="bias%d" % b) for b in range(2)]
-        hb_slots = sb.tile([P, PACK, I], BF16, name="hb_slots", align_bytes=64)
-        for b in range(2):
-            nc.vector.tensor_reduce(out=peak[b][:], in_=zb[b][:], axis=mybir.AxisListType.X, op=ALU.max)
-        for b in range(2):
-            nc.scalar.activation(bias[b][:], peak[b][:], ACT.Copy, scale=-0.4)
-            for u in range(2):
-                nc.scalar.activation(
-                    hb_slots[:, 2 * b + u, :], zb[b][:, u, :], ACT.Relu, bias=bias[b][:, u : u + 1], scale=1.0
-                )
+        hb = sb.tile([P, I, PACK], BF16, name="hb", tag="reused", align_bytes=64)
+        hb_codes = sb.tile([P, I], U32, name="hb_codes", align_bytes=64)
+        hb_scales = sb.tile([P, I], U8, name="hb_scales", align_bytes=64)
+        nc.vector.tensor_scalar(
+            out=hb[:, :HALF, :].rearrange("p (c e) t -> p c t e", e=4),
+            in0=hb_slots[:, :, :HALF].rearrange("p t (c e) -> p c t e", e=4),
+            scalar1=0.4,
+            scalar2=None,
+            op0=ALU.mult,
+        )
+        nc.scalar.activation(
+            hb[:, HALF:, :].rearrange("p (c e) t -> p c t e", e=2),
+            hb_slots[:, :, HALF:].rearrange("p t (c e) -> p c t e", e=2),
+            ACT.Copy,
+            scale=0.4,
+        )
 
         ha = [sb.tile([P, HALF, PACK], BF16, name="ha%d" % h, align_bytes=64) for h in range(2)]
         ha_codes = [sb.tile([P, HALF], U32, name="ha_codes%d" % h, align_bytes=64) for h in range(2)]
         ha_scales = [sb.tile([P, HALF], U8, name="ha_scales%d" % h, align_bytes=64) for h in range(2)]
         for h in range(2):
             nc.vector.tensor_tensor(
-                out=ha[h][:],
-                in0=za[h][:].rearrange("p t j -> p j t"),
-                in1=tf_picked[:, :, HALF * h : HALF * (h + 1)].rearrange("p t j -> p j t"),
+                out=ha[h][:].rearrange("p (c e) t -> p c t e", e=2),
+                in0=za[h][:].rearrange("p t (c e) -> p c t e", e=2),
+                in1=tf_picked[:, :, HALF * h : HALF * (h + 1)].rearrange("p t (c e) -> p c t e", e=2),
                 op=ALU.mult,
-            )
-        hb = sb.tile([P, I, PACK], BF16, name="hb", align_bytes=64)
-        hb_codes = sb.tile([P, I], U32, name="hb_codes", align_bytes=64)
-        hb_scales = sb.tile([P, I], U8, name="hb_scales", align_bytes=64)
-        nc.vector.tensor_copy(out=hb[:], in_=hb_slots[:].rearrange("p t i -> p i t"))
-        for h in range(2):
-            nc.vector.quantize_mx(
-                out=ha_codes[h][:].bitcast(E5M2), scales=ha_scales[h][:], in_=ha[h][:].rearrange("p j t -> p (j t)")
             )
         nc.vector.quantize_mx(
             out=hb_codes[:].bitcast(E4M3), scales=hb_scales[:], in_=hb[:].rearrange("p i t -> p (i t)")
         )
+        for h in range(2):
+            nc.vector.quantize_mx(
+                out=ha_codes[h][:].bitcast(E5M2), scales=ha_scales[h][:], in_=ha[h][:].rearrange("p j t -> p (j t)")
+            )
 
         a0 = [ps.tile([P, I], F32, name="a0_%d" % h) for h in range(2)]
         weighted = [sb.tile([P, S, I // S], F32, name="weighted%d" % h) for h in range(2)]

from contextlib import ExitStack

import concourse.mybir as mybir

K, T, J, I, R, C, S = 512, 512, 256, 256, 512, 512, 64
FLOPS = 2 * K * R * J + 2 * K * R * I + 2 * R * J * I

F32 = mybir.dt.float32
BF16 = mybir.dt.bfloat16
I32 = mybir.dt.int32
U32 = mybir.dt.uint32
U16 = mybir.dt.uint16
U8 = mybir.dt.uint8
E4M3 = mybir.dt.float8_e4m3fn_x4
E5M2 = mybir.dt.float8_e5m2_x4
E2M1 = mybir.dt.float4_e2m1fn_x4
ALU = mybir.AluOpType
ACT = mybir.ActivationFunctionType

P = 128
PACK = 4
RUN = 8
HALF = 128


def tile_list_meet_timestable_peakgated_summed_kernel(
    tc, xt_words, xt_scales, wa_words, wa_scales, tf, wb_words, wb_scales, cw1, offs, offs2, offs3, out
):
    nc = tc.nc
    with ExitStack() as ctx:
        lists = ctx.enter_context(tc.tile_pool(name="lists", bufs=1))
        sb = ctx.enter_context(tc.tile_pool(name="sb", bufs=1))
        ps = ctx.enter_context(tc.psum_pool(name="ps", bufs=1))

        def load_scale_rows(queue, plane, scales):
            rows = scales[0].bitcast(I32)
            for q in range(4):
                queue.dma_start(out=plane[32 * q : 32 * q + 4, :].bitcast(I32), in_=rows[4 * q : 4 * q + 4, :])

        def deal(dst, src, run):
            nc.vector.tensor_copy(
                out=dst[:].bitcast(I32).rearrange("p (t q s) -> p t q s", t=PACK, s=run),
                in_=src[:].bitcast(I32).rearrange("p (q t s) -> p t q s", t=PACK, s=run),
            )

        list_a = lists.tile([P, J // 16], U16, name="list_a")
        list_f = lists.tile([P, J // 16], U16, name="list_f")
        list_b = lists.tile([P, I // 16], U16, name="list_b")

        xs = sb.tile([P, T], U8, name="xs", align_bytes=64)
        wbs_raw = sb.tile([P, R], U8, name="wbs_raw", align_bytes=64)
        was_raw = sb.tile([P, R], U8, name="was_raw", tag="reused", align_bytes=64)

        nc.gpsimd.memset(xs[:].bitcast(I32), 0)
        nc.vector.memset(wbs_raw[:].bitcast(I32), 0)
        nc.vector.memset(was_raw[:].bitcast(I32), 0)

        xw = sb.tile([P, T], U32, name="xw", align_bytes=64)
        wbw_raw = sb.tile([P, 2 * R], U8, name="wbw_raw", align_bytes=64)
        waw_raw = sb.tile([P, R], U32, name="waw_raw", align_bytes=64)
        tf_rows = [sb.tile([P, C], F32, name="tf_rows%d" % t, align_bytes=64) for t in range(PACK)]
        cw = sb.tile([P, I], F32, name="cw", align_bytes=64)

        nc.sync.dma_start(list_b[:], offs3)
        tf_by_slot = tf.rearrange("(q t s) c -> t q s c", t=PACK, s=RUN)
        for t in range(2):
            nc.gpsimd.dma_start(out=tf_rows[t][:], in_=tf_by_slot[t])
        nc.sync.dma_start(out=xw[:].bitcast(I32), in_=xt_words[0].rearrange("p n t -> p (n t)").bitcast(I32))
        load_scale_rows(nc.scalar, xs, xt_scales)
        nc.sync.dma_start(list_a[:], offs)
        nc.sync.dma_start(list_f[:], offs2)
        load_scale_rows(nc.sync, wbs_raw, wb_scales)
        nc.sync.dma_start(out=wbw_raw[:].bitcast(I32), in_=wb_words[0].bitcast(I32))
        nc.sync.dma_start(out=tf_rows[2][:], in_=tf_by_slot[2])
        nc.sync.dma_start(out=waw_raw[:].bitcast(I32), in_=wa_words[0].rearrange("p n t -> p (n t)").bitcast(I32))
        nc.sync.dma_start(out=tf_rows[3][:], in_=tf_by_slot[3])
        load_scale_rows(nc.sync, was_raw, wa_scales)
        nc.sync.dma_start(out=cw[:], in_=cw1[0].partition_broadcast(P))

        xw_b = sb.tile([P, I], U32, name="xw_b", align_bytes=64)
        xs_b = sb.tile([P, I], U8, name="xs_b", align_bytes=64)
        nc.vector.tensor_copy(xw_b[:], xw[:].indirect(list_b[:]))
        nc.vector.tensor_copy(xs_b[:], xs[:].indirect(list_b[:]))
        wbw = sb.tile([P, 2 * R], U8, name="wbw", align_bytes=64)
        wbs = sb.tile([P, R], U8, name="wbs", tag="reused2", align_bytes=64)
        deal(wbw, wbw_raw, RUN // 2)
        deal(wbs, wbs_raw, RUN // 4)
        zb = [ps.tile([P, I], F32, name="zb%d" % t) for t in range(PACK)]
        for t in range(PACK):
            nc.tensor.matmul_mx(
                out=zb[t][:],
                lhsT=wbw[:, 2 * P * t : 2 * P * (t + 1)].bitcast(E2M1),
                lhsT_scale=wbs[:, P * t : P * (t + 1)],
                rhs=xw_b[:].bitcast(E5M2),
                rhs_scale=xs_b[:],
                start=True,
                stop=True,
            )

        xw_a = sb.tile([P, J], U32, name="xw_a", align_bytes=64)
        xs_a = sb.tile([P, J], U8, name="xs_a", align_bytes=64)
        nc.vector.tensor_copy(xw_a[:], xw[:].indirect(list_a[:]))
        nc.vector.tensor_copy(xs_a[:], xs[:].indirect(list_a[:]))
        waw = sb.tile([P, R], U32, name="waw", align_bytes=64)
        deal(waw, waw_raw, RUN)
        tf_picked = sb.tile([P, PACK, J], F32, name="tf_picked", align_bytes=64)
        for t in range(2):
            nc.scalar.activation(tf_picked[:, t, :], tf_rows[t][:].indirect(list_f[:]), ACT.Copy)

        neg_peak = [tf_picked[:, 2, 0:1], tf_picked[:, 3, 0:1], tf_picked[:, 2, 128:129], tf_picked[:, 3, 128:129]]
        hb_slots = sb.tile([P, PACK, I], F32, name="hb_slots", align_bytes=64)
        for t in range(PACK):
            nc.vector.tensor_reduce(
                out=neg_peak[t], in_=zb[t][:], axis=mybir.AxisListType.X, op=ALU.max, negate=True
            )
            nc.scalar.activation(hb_slots[:, t, :], zb[t][:], ACT.Relu, bias=neg_peak[t], scale=2.5)
        for h in range(2):
            for t in range(2, PACK):
                nc.scalar.activation(
                    tf_picked[:, t, HALF * h : HALF * (h + 1)],
                    tf_rows[t][:].indirect(list_f[:, 8 * h : 8 * (h + 1)]),
                    ACT.Copy,
                )

        was = sb.tile([P, R], U8, name="was", tag="reused2", align_bytes=64)
        deal(was, was_raw, RUN // 4)
        za = [ps.tile([P, PACK, HALF], F32, name="za%d" % h) for h in range(2)]
        for h in range(2):
            cols = slice(HALF * h, HALF * (h + 1))
            for t in range(PACK):
                nc.tensor.matmul_mx(
                    out=za[h][:, t, :],
                    lhsT=waw[:, P * t : P * (t + 1)].bitcast(E4M3),
                    lhsT_scale=was[:, P * t : P * (t + 1)],
                    rhs=xw_a[:, cols].bitcast(E5M2),
                    rhs_scale=xs_a[:, cols],
                    start=True,
                    stop=True,
                )

        hb = sb.tile([P, I, PACK], BF16, name="hb", tag="reused", align_bytes=64)
        hb_codes = sb.tile([P, I], U32, name="hb_codes", align_bytes=64)
        hb_scales = sb.tile([P, I], U8, name="hb_scales", align_bytes=64)
        nc.vector.tensor_scalar(
            out=hb[:, :HALF, :].rearrange("p (c e) t -> p c t e", e=4),
            in0=hb_slots[:, :, :HALF].rearrange("p t (c e) -> p c t e", e=4),
            scalar1=0.4,
            scalar2=None,
            op0=ALU.mult,
        )
        nc.scalar.activation(
            hb[:, HALF:, :].rearrange("p (c e) t -> p c t e", e=2),
            hb_slots[:, :, HALF:].rearrange("p t (c e) -> p c t e", e=2),
            ACT.Copy,
            scale=0.4,
        )

        ha = [sb.tile([P, HALF, PACK], BF16, name="ha%d" % h, align_bytes=64) for h in range(2)]
        ha_codes = [sb.tile([P, HALF], U32, name="ha_codes%d" % h, align_bytes=64) for h in range(2)]
        ha_scales = [sb.tile([P, HALF], U8, name="ha_scales%d" % h, align_bytes=64) for h in range(2)]
        for h in range(2):
            nc.vector.tensor_tensor(
                out=ha[h][:].rearrange("p (c e) t -> p c t e", e=2),
                in0=za[h][:].rearrange("p t (c e) -> p c t e", e=2),
                in1=tf_picked[:, :, HALF * h : HALF * (h + 1)].rearrange("p t (c e) -> p c t e", e=2),
                op=ALU.mult,
            )
        nc.vector.quantize_mx(
            out=hb_codes[:].bitcast(E4M3), scales=hb_scales[:], in_=hb[:].rearrange("p i t -> p (i t)")
        )
        for h in range(2):
            nc.vector.quantize_mx(
                out=ha_codes[h][:].bitcast(E5M2), scales=ha_scales[h][:], in_=ha[h][:].rearrange("p j t -> p (j t)")
            )

        a0 = [ps.tile([P, I], F32, name="a0_%d" % h) for h in range(2)]
        weighted = [sb.tile([P, S, I // S], F32, name="weighted%d" % h) for h in range(2)]
        res = [sb.tile([P, S], F32, name="res%d" % h) for h in range(2)]
        for h in range(2):
            nc.tensor.matmul_mx(
                out=a0[h][:],
                lhsT=ha_codes[h][:].bitcast(E5M2),
                lhsT_scale=ha_scales[h][:],
                rhs=hb_codes[:].bitcast(E4M3),
                rhs_scale=hb_scales[:],
                start=True,
                stop=True,
            )
        for h in range(2):
            nc.vector.scalar_tensor_tensor(
                out=weighted[h][:].rearrange("p s u -> p (s u)"),
                in0=a0[h][:],
                scalar=0.04,
                in1=cw[:],
                op0=ALU.mult,
                op1=ALU.mult,
            )
        for h in range(2):
            nc.vector.tensor_reduce(out=res[h][:], in_=weighted[h][:], axis=mybir.AxisListType.X, op=ALU.add)
            nc.sync.dma_start(out=out[HALF * h : HALF * (h + 1), :], in_=res[h][:])
